import numpy as np
CORES = [13,21,141,149]
N = 4
T, FF, CAPT = 2048, 32, 2048
def entries(a): return a.T.reshape(-1)
def pack(v, P): return np.ascontiguousarray(np.asarray(v, np.int32).reshape(-1, P).T)
def lists(rng, how):
    w = rng.random(N) ** 2 + 1e-3; c = T // 8 + ((CAPT - N * (T // 8)) * w / w.sum()).astype(np.int64)
    a = rng.permutation(N)
    if how == "few": c = np.zeros(N, np.int64); c[N - 1] = 3; c[int(rng.integers(N - 1))] = 1
    if how == "lone": s = int(rng.integers(CAPT - T + 1)); c = np.zeros(N, np.int64); c[a[0]] = T; c[a[1]] = s; c[a[2]] = CAPT - T - s
    if how == "none": c = np.zeros(N, np.int64)
    if how == "pair": s = 2 * int(rng.integers(512, 767)) + 1; c = np.zeros(N, np.int64); c[a[0]] = s; c[a[1]] = CAPT - s - 1; c[a[2]] = 1
    if how == "zeros": c = np.full(N, 2); c[0] = T - 7 - 2 * int(rng.integers(T // 16))
    K = np.stack([rng.permutation(np.arange(T) < c[r]) for r in range(N)])
    if how == "zeros": K = np.stack([np.r_[True, rng.permutation(np.arange(T - 2) < c[r] - 2), True] for r in range(N)])
    return {"keep": np.stack([pack(k, 16) for k in K])}
def blank(d):
    for r in range(N):
        k = entries(d["keep"][r]); d["x"][r][:, np.nonzero(k)[0][1:-1:4]] = 0; d["x"][r][:, np.nonzero(1 - k)[0][::4]] = 0
def setup_inputs(rng):
    return dict({"x": rng.standard_normal((N, 128, T), dtype=np.float32), "w1": np.repeat((rng.standard_normal((1, 128, FF * 128), dtype=np.float32) / 8), N, axis=0), "w2": np.repeat((rng.standard_normal((1, 128, FF * 128), dtype=np.float32) / 64), N, axis=0)}, **lists(rng, "uniform"))
def setup_inputs_few(rng):
    d = setup_inputs(rng); d.update(lists(rng, "few"))
    for k in ("x",): d[k] = (d[k].astype(np.float32) * 1024.0).astype(d[k].dtype)
    return d
def setup_inputs_lone(rng):
    d = setup_inputs(rng); d.update(lists(rng, "lone"))
    for k in ("x",): d[k] = (d[k].astype(np.float32) * (1 / 1024.0)).astype(d[k].dtype)
    return d
def setup_inputs_none(rng):
    d = setup_inputs(rng); d.update(lists(rng, "none"))
    return d
def setup_inputs_pair(rng):
    d = setup_inputs(rng); d.update(lists(rng, "pair"))
    return d
def setup_inputs_zeros(rng):
    d = setup_inputs(rng); d.update(lists(rng, "zeros"))
    blank(d)
    return d
def check_inputs(x):
    bad = []
    if x["keep"].min() < 0 or x["keep"].max() >= 2: bad.append("keep out of range")
    if int(x["keep"].sum()) > CAPT: bad.append("more than CAPT tokens are kept in all")
    if any((x[k] != x[k][:1]).any() for k in ("w1", "w2")): bad.append("w1 or w2 is not alike on all ranks")
    return bad
def reference(x, w1, w2, keep):
    X, W1, W2 = x.astype(np.float64), w1.astype(np.float64), w2.astype(np.float64)
    Y = X.copy()
    for r in range(N):
        P = np.nonzero(entries(keep[r]) == 1)[0]
        if len(P) == 0: continue
        Y[r][:, P] = sum(W2[r][:, 128 * f:128 * f + 128].T @ np.maximum(W1[r][:, 128 * f:128 * f + 128].T @ X[r][:, P], 0.0) for f in range(FF))
    return {"y": Y.astype(np.float32)}

@@ -1,0 +1,299 @@
+from concourse.bass import DstId, RemoteDMATransfer
+from concourse.mybir import dt, AluOpType, ActivationFunctionType
+
+NCORES = 256
+SLOTS, PER, NT = 2048, 128, 2048
+CH = 16
+X0 = 4
+
+SCRATCH = {
+    "wbuf": ("sbuf", [128, CH, 512], "float32"),
+    "win": ("sbuf", [128, X0 + NT + SLOTS], "float32"),
+    "xc": ("sbuf", [128, SLOTS], "float32"),
+    "ysb": ("sbuf", [128, NT], "float32"),
+    "xin": ("sbuf", [128, 2, PER], "float32"),
+    "xs": ("sbuf", [128, PER], "float32"),
+    "hid": ("sbuf", [128, CH * 256], "float32"),
+    "outr": ("sbuf", [128, PER], "float32"),
+    "ki": ("sbuf", [128, 128], "int32"), "kb": ("sbuf", [128, 128], "bfloat16"),
+    "pi32": ("sbuf", [128, 1], "int32"), "pm32": ("sbuf", [128, 1], "int32"),
+    "pmf": ("sbuf", [128, 1], "float32"), "initc": ("sbuf", [128, 1], "float32"),
+    "m0": ("sbuf", [128, 1], "float32"), "m1": ("sbuf", [128, 1], "float32"),
+    "offp": ("sbuf", [128, 2], "uint16"), "o8": ("sbuf", [128, 16], "uint16"),
+    "offs": ("sbuf", [128, 128], "uint16"), "posu": ("sbuf", [128, 128], "uint16"),
+    "dm": ("sbuf", [128, 128], "float32"), "jb": ("sbuf", [128, 128], "float32"), "jj": ("sbuf", [128, 128], "float32"),
+    "c16": ("sbuf", [128, 128], "float32"), "sc": ("sbuf", [128, 128], "float32"), "t2": ("sbuf", [128, 128], "float32"),
+    "t3": ("sbuf", [128, 128], "float32"), "pos": ("sbuf", [128, 128], "float32"),
+    "mone": ("sbuf", [128, 128], "bfloat16"), "md": ("sbuf", [128, 128], "bfloat16"), "mr": ("sbuf", [128, 128], "bfloat16"),
+    "vhi": ("sbuf", [128, 256], "bfloat16"), "vlo": ("sbuf", [128, 256], "bfloat16"),
+    "va": ("sbuf", [128, 256], "bfloat16"), "vb": ("sbuf", [128, 256], "bfloat16"), "val": ("sbuf", [128, 256], "bfloat16"),
+    "sel": ("sbuf", [128, 16 * 128], "bfloat16"),
+    "dw": ("sbuf", [128, NT + SLOTS], "bfloat16"),
+}
+for _k in range(8):
+    SCRATCH["ps%d" % _k] = ("psum", [128, 512], "float32")
+
+SEMAPHORES = (["gi", "v", "p1", "p2", "kl", "xl", "go", "tl", "th", "tsent", "gv0", "gv1", "gs0", "gs1", "posr",
+               "xsr", "l1a", "l1b", "ha", "hb", "acc", "rdy", "rsent", "res", "fv0", "fv1", "fs0", "fs1", "ys", "fsent"]
+              + ["ld%d" % k for k in range(CH // 2)] + ["snt%d" % k for k in range(CH // 2)]
+              + ["w%d" % k for k in range(CH)])
+
+
+def bits(mask):
+    return [e for e in range(16) if (mask >> e) & 1]
+
+
+def mask_of(engines):
+    return sum(1 << e for e in engines)
+
+
+def rank_program(g, core, T, topo):
+    S = T.sem
+    A = AluOpType
+
+    def same_chip(a, b):
+        return topo.host(a) == topo.host(b) and topo.chip(a) == topo.chip(b)
+
+    home = [q for q in T.cores if same_chip(q, core)]
+    if not home:
+        return
+    home = home[0]
+    peer = [q for q in T.cores if topo.same_plane(home, q)][0]
+    lo, hi = min(home, peer), max(home, peer)
+    chip_of = {q: [c for c in range(NCORES) if same_chip(c, q)] for q in (lo, hi)}
+    workers = chip_of[lo] + chip_of[hi]
+    w = workers.index(core)
+    mine = chip_of[home]
+    near = [c for c in mine if c != home and topo.die(c) == topo.die(home)]
+    far = [c for c in mine if topo.die(c) != topo.die(home)]
+    is_rank = core == home
+    carrier = [near[(c // 2) % len(near)] if c % 2 == 0 else far[(c // 2) % len(far)] for c in range(CH)]
+
+    on = bits(topo.mask(core, [c for c in mine if c != core][0]))
+    off = bits(topo.mask(core, peer if is_rank else [q for q in (lo, hi) if q != home][0]))
+    on_rest = [e for e in on if e not in off]
+    on_a, on_b = on[0::2], on[1::2]
+
+    def tr(src, dests, engines, sem):
+        ids = []
+        for d, _ in dests:
+            rid, pid = topo.addr(d, core)
+            ids.append(DstId(rid=rid, pnc=pid))
+        return RemoteDMATransfer(dst_ids=ids, dma_engine_mask=mask_of(engines), remote_sem=sem,
+                                 srcs=[src], dsts=[ap for _, ap in dests], alu_op=0)
+
+    R0 = X0 + NT
+
+    def res_slot(i):
+        return T.win[:, R0 + i * PER:R0 + (i + 1) * PER]
+
+    V = g.vector
+    PE = g.tensor
+    vn = [0]
+
+    def vinc(call):
+        call.then_inc(S.v, 1)
+        vn[0] += 1
+
+    def vwait():
+        V.wait_ge(S.v, vn[0])
+
+    if is_rank:
+        low = core == lo
+        sg = 1.0 if low else -1.0
+        cb = SLOTS if low else 2 * SLOTS - 1
+        g.sync.dma_start(T.ki[0:16, :], T.keep[:, :]).then_inc(S.kl, 16)
+
+        def load(k, qa, qb):
+            qa.dma_start(T.wbuf[:, 2 * k:2 * k + 2, 0:256], T.w1[:, 512 * k:512 * k + 512]).then_inc(S["ld%d" % k], 16)
+            qb.dma_start(T.wbuf[:, 2 * k:2 * k + 2, 256:512], T.w2[:, 512 * k:512 * k + 512]).then_inc(S["ld%d" % k], 16)
+
+        load(0, g.sync, g.scalar)
+        g.sync.dma_start(T.win[:, X0:X0 + NT // 2], T.x[:, 0:NT // 2]).then_inc(S.xl, 16)
+        g.scalar.dma_start(T.win[:, X0 + NT // 2:X0 + NT], T.x[:, NT // 2:NT]).then_inc(S.xl, 16)
+        load(1, g.sync, g.scalar)
+        load(2, g.sync, g.scalar)
+
+        g.iota(T.pi32[:, :], [[0, 1]], 0, 1).then_inc(S.gi, 1)
+        g.iota(T.dm[0:16, :], [[0, 8], [1, 16]], 0, -1, allow_small_or_imprecise_dtypes=True).then_inc(S.gi, 1)
+        g.iota(T.jb[:, :], [[16, 128]], 0, 0, allow_small_or_imprecise_dtypes=True).then_inc(S.gi, 1)
+        g.iota(T.vhi[:, :], [[64, 4], [0, 64]], 0, 16, allow_small_or_imprecise_dtypes=True).then_inc(S.gi, 1)
+        g.iota(T.vlo[:, :], [[0, 4], [1, 64]], 1, 0, allow_small_or_imprecise_dtypes=True).then_inc(S.gi, 1)
+        vinc(V.memset(T.mone[0:16, :], sg))
+        vinc(V.memset(T.c16[:, :], -16.0))
+        vinc(V.memset(T.win[:, 0:X0], 0.0))
+        vinc(V.memset(T.sel[:, :], 0.0))
+        vinc(V.memset(T.dw[:, NT:NT + SLOTS], 0.0))
+        V.wait_ge(S.gi, 5)
+        vwait()
+        vinc(V.tensor_scalar(T.pm32[:, :], T.pi32[:, :], 15, None, A.bitwise_and))
+        vinc(V.tensor_copy(T.offp[:, 0:1], T.pi32[:, :]))
+        vinc(V.tensor_scalar(T.md[0:16, :], T.dm[0:16, :], 0.0, -sg, A.is_le, A.mult))
+        vinc(V.tensor_scalar(T.mr[0:16, :], T.dm[0:16, :], 0.0, None, A.is_equal))
+        for q in range(8):
+            vinc(V.memset(T.sel[:, 16 * q:16 * q + 129 * 15 + 1:129], 1.0))
+        vwait()
+        vinc(V.tensor_copy(T.pmf[:, :], T.pm32[:, :]))
+        vinc(V.tensor_scalar(T.initc[:, :], T.pm32[:, :], -1.0, float(cb + 16), A.mult, A.add))
+        vinc(V.tensor_scalar(T.m0[:, :], T.pm32[:, :], 0.0, None, A.is_equal))
+        vinc(V.tensor_scalar(T.m1[:, :], T.pm32[:, :], 1.0, None, A.is_equal))
+        V.wait_ge(S.kl, 16)
+        vwait()
+        vinc(V.tensor_copy(T.kb[0:16, :], T.ki[0:16, :]))
+        kb_at = vn[0]
+        PE.wait_ge(S.v, kb_at)
+        PE.matmul(T.ps5[:, 0:128], T.mone[0:16, :], T.kb[0:16, :], True, True).then_inc(S.p1, 1)
+        PE.matmul(T.ps6[:, 0:128], T.md[0:16, :], T.kb[0:16, :], True, True).then_inc(S.p1, 1)
+        PE.matmul(T.ps7[:, 0:128], T.mr[0:16, :], T.kb[0:16, :], True, True).then_inc(S.p1, 1)
+        vwait()
+        V.wait_ge(S.p1, 3)
+        vinc(V.tensor_tensor_scan(T.sc[:, :], T.ps5[:, 0:128], T.c16[:, :], T.initc[:, 0:1], A.add, A.add))
+        vinc(V.tensor_scalar(T.jj[:, :], T.jb[:, :], T.pmf[:, 0:1], None, A.add))
+        vwait()
+        vinc(V.tensor_tensor(T.t2[:, :], T.sc[:, :], T.ps6[:, 0:128], A.add))
+        vinc(V.tensor_scalar(T.va[:, :], T.vhi[:, :], T.m0[:, 0:1], None, A.mult))
+        vinc(V.tensor_scalar(T.vb[:, :], T.vlo[:, :], T.m1[:, 0:1], None, A.mult))
+        vwait()
+        vinc(V.tensor_tensor(T.t3[:, :], T.t2[:, :], T.ps7[:, 0:128], A.mult))
+        vinc(V.tensor_tensor(T.val[:, :], T.va[:, :], T.vb[:, :], A.add))
+        vwait()
+        vinc(V.tensor_tensor(T.pos[:, :], T.t3[:, :], T.jj[:, :], A.add))
+        vwait()
+        vinc(V.tensor_copy(T.o8[:, :], T.pos[:, :].indirect(T.offp[:, 0:1])))
+        vwait()
+        vinc(V.tensor_copy(T.dw[:, :].indirect(T.o8[:, :]), T.val[:, :]))
+        PE.wait_ge(S.v, vn[0])
+        for a in range(16):
+            mm = PE.matmul(T.ps4[:, 0:128], T.sel[:, 128 * a:128 * a + 128], T.dw[:, NT + a:NT + SLOTS:16], a == 0, a == 15)
+        mm.then_inc(S.p2, 1)
+        vwait()
+        V.wait_ge(S.p2, 1)
+        vinc(V.tensor_copy(T.offs[:, :], T.ps4[:, 0:128]))
+        offs_at = vn[0]
+        vwait()
+        V.wait_ge(S.xl, 32)
+        g.scalar.wait_ge(S.v, offs_at)
+        g.scalar.wait_ge(S.xl, 32)
+        peer_half = SLOTS // 2 if low else 0
+        own_half = SLOTS // 2 - peer_half
+        src = T.win[:, X0 - 1:X0 + NT]
+        for i, base in enumerate((peer_half, own_half)):
+            b, c = base, base + 512
+            V.tensor_copy(T.xc[:, b:b + 512], src.indirect(T.offs[:, b // 16:b // 16 + 32])).then_inc(S["gv%d" % i], 1)
+            g.scalar.activation(T.xc[:, c:c + 512], src.indirect(T.offs[:, c // 16:c // 16 + 32]),
+                                ActivationFunctionType.Copy).then_inc(S["gs%d" % i], 1)
+        snt_used = []
+
+        def send(k):
+            g.wait_ge(S["ld%d" % k], 32)
+            c0, c1 = 2 * k, 2 * k + 1
+            g.remote_dma_fused([tr(T.wbuf[:, c0, :], [(carrier[c0], T.wbuf[:, c0, :])], on_b, S["w%d" % c0]),
+                                tr(T.wbuf[:, c1, :], [(carrier[c1], T.wbuf[:, c1, :])], on_a, S["w%d" % c1])],
+                               local_sem=S["snt%d" % k])
+
+        half = 0 if low else 1
+        tsem = S.tl if low else S.th
+
+        def tok(dests, engines):
+            ts = []
+            for d, e in zip(dests, engines):
+                i = workers.index(d)
+                ts.append(tr(T.xc[:, i * PER:(i + 1) * PER], [(d, T.xin[:, half, :])], [e], tsem))
+            g.remote_dma_fused(ts, local_sem=S.tsent)
+            return len(ts)
+
+        send(0)
+        g.wait_ge(S.gv0, 1)
+        g.wait_ge(S.gs0, 1)
+        nt = tok(chip_of[peer], off)
+        g.wait_ge(S.gv1, 1)
+        g.wait_ge(S.gs1, 1)
+        nt += tok(far + near, on_rest[0::2] + on_rest[1::2])
+        for k in range(1, CH // 2):
+            send(k)
+        for k in range(3, CH // 2):
+            g.sync.wait_ge(S["snt%d" % (k - 2)], 16)
+            load(k, g.sync, g.sync)
+        V.wait_ge(S.gv1, 1)
+        V.wait_ge(S.gs1, 1)
+        vinc(V.tensor_copy(T.posu[:, :], T.pos[:, :]))
+        V.wait_ge(S.th if low else S.tl, 1)
+        V.tensor_tensor(T.xs[:, :], T.xc[:, w * PER:(w + 1) * PER], T.xin[:, 1 - half, :], A.add).then_inc(S.xsr, 1)
+        vwait()
+    else:
+        n = 0
+        for c in range(CH):
+            if carrier[c] != core:
+                continue
+            g.wait_ge(S["w%d" % c], len(on_a))
+            rest = [d for d in mine if d not in (core, home)]
+            a = [d for d in rest if topo.die(d) != topo.die(core)]
+            b = [d for d in rest if topo.die(d) == topo.die(core)]
+            ap = T.wbuf[:, c, :]
+            g.remote_dma_fused([tr(ap, [(d, ap) for d in a], on_a, S["w%d" % c]),
+                                tr(ap, [(d, ap) for d in b], on_b, S["w%d" % c])], local_sem=S.fsent)
+            n += len(on_a) + len(on_b)
+        V.wait_ge(S.tl, 1)
+        V.wait_ge(S.th, 1)
+        V.tensor_tensor(T.xs[:, :], T.xin[:, 0, :], T.xin[:, 1, :], A.add).then_inc(S.xsr, 1)
+
+    PE.wait_ge(S.xsr, 1)
+    l1 = (S.l1a, S.l1b)
+    hs = (S.ha, S.hb)
+
+    def layer1(c):
+        if is_rank:
+            PE.wait_ge(S["ld%d" % (c // 2)], 32)
+        else:
+            PE.wait_ge(S["w%d" % c], len(on_a))
+        ps = T["ps%d" % (c % 4)]
+        PE.matmul(ps[:, 0:128], T.wbuf[:, c, 0:128], T.xs[:, :], True, True)
+        PE.matmul(ps[:, 128:256], T.wbuf[:, c, 128:256], T.xs[:, :], True, True).then_inc(l1[c % 2], 1)
+        V.wait_ge(l1[c % 2], c // 2 + 1)
+        V.tensor_scalar(T.hid[:, 256 * c:256 * c + 256], ps[:, 0:256], 0.0, None, A.max).then_inc(hs[c % 2], 1)
+
+    layer1(0)
+    for c in range(CH):
+        if c + 1 < CH:
+            layer1(c + 1)
+        PE.wait_ge(hs[c % 2], c // 2 + 1)
+        for i in (0, 1):
+            mm = PE.matmul(T.ps4[:, 0:128], T.wbuf[:, c, 256 + 128 * i:384 + 128 * i],
+                           T.hid[:, 256 * c + 128 * i:256 * c + 128 * i + 128], c == 0 and i == 0, c == CH - 1 and i == 1)
+    mm.then_inc(S.acc, 1)
+
+    V.wait_ge(S.acc, 1)
+    out = res_slot(w) if is_rank else T.outr[:, :]
+    V.tensor_copy(out, T.ps4[:, 0:128]).then_inc(S.rdy, 1)
+    g.wait_ge(S.rdy, 1)
+    other = peer
+    if is_rank:
+        g.remote_dma_fused([tr(out, [(other, res_slot(w))], off, S.res)], local_sem=S.rsent)
+        g.wait_ge(S.rsent, len(off))
+        g.wait_ge(S.tsent, nt)
+        for k in [0] + list(range(CH // 2 - 2, CH // 2)):
+            g.wait_ge(S["snt%d" % k], 16)
+        total = 7 * len(on_rest) + 8 * len(off)
+        yw = T.win[:, X0:X0 + NT + SLOTS]
+        V.wait_ge(S.res, total)
+        V.wait_ge(S.rdy, 1)
+        g.scalar.wait_ge(S.res, total)
+        g.scalar.wait_ge(S.rdy, 1)
+        g.scalar.wait_ge(S.v, vn[0])
+        for i in (0, 1):
+            b, c = 512 * i, 1024 + 512 * i
+            V.tensor_copy(T.ysb[:, b:b + 512], yw.indirect(T.posu[:, b // 16:b // 16 + 32])).then_inc(S["fv%d" % i], 1)
+            g.scalar.activation(T.ysb[:, c:c + 512], yw.indirect(T.posu[:, c // 16:c // 16 + 32]),
+                                ActivationFunctionType.Copy).then_inc(S["fs%d" % i], 1)
+        for i in (0, 1):
+            b, c = 512 * i, 1024 + 512 * i
+            g.sync.wait_ge(S["fv%d" % i], 1)
+            g.sync.dma_start(T.y[:, b:b + 512], T.ysb[:, b:b + 512]).then_inc(S.ys, 16)
+            g.sync.wait_ge(S["fs%d" % i], 1)
+            g.sync.dma_start(T.y[:, c:c + 512], T.ysb[:, c:c + 512]).then_inc(S.ys, 16)
+        g.sync.wait_ge(S.ys, 64)
+    else:
+        g.remote_dma_fused([tr(out, [(other, res_slot(w))], off, S.res),
+                            tr(out, [(home, res_slot(w))], on_rest, S.res)], local_sem=S.rsent)
+        g.wait_ge(S.rsent, len(off) + len(on_rest))
+        g.wait_ge(S.fsent, n)

@@ -3,8 +3,13 @@ from concourse.mybir import dt, AluOpType, ActivationFunctionType
 
 NCORES = 256
 SLOTS, PER, NT = 2048, 128, 2048
+HP = PER // 2
 CH = 16
+PRE = 2
+GATE = 2
+LATE = 3
 X0 = 4
+YP = 512
 
 SCRATCH = {
     "wbuf": ("sbuf", [128, CH, 512], "float32"),
@@ -14,27 +19,30 @@ SCRATCH = {
     "xin": ("sbuf", [128, 2, PER], "float32"),
     "xs": ("sbuf", [128, PER], "float32"),
     "hid": ("sbuf", [128, CH * 256], "float32"),
-    "outr": ("sbuf", [128, PER], "float32"),
+    "out0": ("sbuf", [128, HP], "float32"), "out1": ("sbuf", [128, HP], "float32"),
     "ki": ("sbuf", [128, 128], "int32"), "kb": ("sbuf", [128, 128], "bfloat16"),
     "pi32": ("sbuf", [128, 1], "int32"), "pm32": ("sbuf", [128, 1], "int32"),
     "pmf": ("sbuf", [128, 1], "float32"), "initc": ("sbuf", [128, 1], "float32"),
     "m0": ("sbuf", [128, 1], "float32"), "m1": ("sbuf", [128, 1], "float32"),
+    "vh4": ("sbuf", [128, 4], "float32"), "vhm": ("sbuf", [128, 4], "float32"),
     "offp": ("sbuf", [128, 2], "uint16"), "o8": ("sbuf", [128, 16], "uint16"),
     "offs": ("sbuf", [128, 128], "uint16"), "posu": ("sbuf", [128, 128], "uint16"),
     "dm": ("sbuf", [128, 128], "float32"), "jb": ("sbuf", [128, 128], "float32"), "jj": ("sbuf", [128, 128], "float32"),
     "c16": ("sbuf", [128, 128], "float32"), "sc": ("sbuf", [128, 128], "float32"), "t2": ("sbuf", [128, 128], "float32"),
     "t3": ("sbuf", [128, 128], "float32"), "pos": ("sbuf", [128, 128], "float32"),
     "mone": ("sbuf", [128, 128], "bfloat16"), "md": ("sbuf", [128, 128], "bfloat16"), "mr": ("sbuf", [128, 128], "bfloat16"),
-    "vhi": ("sbuf", [128, 256], "bfloat16"), "vlo": ("sbuf", [128, 256], "bfloat16"),
-    "va": ("sbuf", [128, 256], "bfloat16"), "vb": ("sbuf", [128, 256], "bfloat16"), "val": ("sbuf", [128, 256], "bfloat16"),
+    "vlo": ("sbuf", [128, 256], "bfloat16"), "val": ("sbuf", [128, 256], "bfloat16"),
+    "one16": ("sbuf", [128, 16], "bfloat16"),
     "sel": ("sbuf", [128, 16 * 128], "bfloat16"),
     "dw": ("sbuf", [128, NT + SLOTS], "bfloat16"),
 }
 for _k in range(8):
     SCRATCH["ps%d" % _k] = ("psum", [128, 512], "float32")
 
-SEMAPHORES = (["gi", "v", "p1", "p2", "kl", "xl", "go", "tl", "th", "tsent", "gv0", "gv1", "gs0", "gs1", "posr",
-               "xsr", "l1a", "l1b", "ha", "hb", "acc", "rdy", "rsent", "res", "fv0", "fv1", "fs0", "fs1", "ys", "fsent"]
+SEMAPHORES = (["go", "gi", "gj", "gk", "v", "p1", "p2a", "p2b", "kl", "xl", "dz", "o16", "vab", "selz", "selr", "offa",
+               "offb", "tl", "th", "tsent", "gv0", "gv1", "gs0", "gs1", "xsr", "l1_0", "l1_1", "l1_2", "l1_3",
+               "h_0", "h_1", "h_2", "h_3", "acca", "accb", "rdya", "rdyb", "rsent", "res", "ys", "fsent"]
+              + ["fv%d" % k for k in range(4)] + ["fs%d" % k for k in range(4)]
               + ["ld%d" % k for k in range(CH // 2)] + ["snt%d" % k for k in range(CH // 2)]
               + ["w%d" % k for k in range(CH)])
 
@@ -50,6 +58,7 @@ def mask_of(engines):
 def rank_program(g, core, T, topo):
     S = T.sem
     A = AluOpType
+    COPY, IDENT = ActivationFunctionType.Copy, ActivationFunctionType.Identity
 
     def same_chip(a, b):
         return topo.host(a) == topo.host(b) and topo.chip(a) == topo.chip(b)
@@ -70,7 +79,7 @@ def rank_program(g, core, T, topo):
     carrier = [near[(c // 2) % len(near)] if c % 2 == 0 else far[(c // 2) % len(far)] for c in range(CH)]
 
     on = bits(topo.mask(core, [c for c in mine if c != core][0]))
-    off = bits(topo.mask(core, peer if is_rank else [q for q in (lo, hi) if q != home][0]))
+    off = bits(topo.mask(core, peer))
     on_rest = [e for e in on if e not in off]
     on_a, on_b = on[0::2], on[1::2]
 
@@ -83,11 +92,8 @@ def rank_program(g, core, T, topo):
                                  srcs=[src], dsts=[ap for _, ap in dests], alu_op=0)
 
     R0 = X0 + NT
-
-    def res_slot(i):
-        return T.win[:, R0 + i * PER:R0 + (i + 1) * PER]
-
     V = g.vector
+    SC = g.scalar
     PE = g.tensor
     vn = [0]
 
@@ -108,81 +114,93 @@ def rank_program(g, core, T, topo):
             qa.dma_start(T.wbuf[:, 2 * k:2 * k + 2, 0:256], T.w1[:, 512 * k:512 * k + 512]).then_inc(S["ld%d" % k], 16)
             qb.dma_start(T.wbuf[:, 2 * k:2 * k + 2, 256:512], T.w2[:, 512 * k:512 * k + 512]).then_inc(S["ld%d" % k], 16)
 
-        load(0, g.sync, g.scalar)
+        load(0, g.sync, SC)
         g.sync.dma_start(T.win[:, X0:X0 + NT // 2], T.x[:, 0:NT // 2]).then_inc(S.xl, 16)
-        g.scalar.dma_start(T.win[:, X0 + NT // 2:X0 + NT], T.x[:, NT // 2:NT]).then_inc(S.xl, 16)
-        load(1, g.sync, g.scalar)
-        load(2, g.sync, g.scalar)
+        SC.dma_start(T.win[:, X0 + NT // 2:X0 + NT], T.x[:, NT // 2:NT]).then_inc(S.xl, 16)
+        load(1, g.sync, g.sync)
+        load(2, g.sync, g.sync)
 
+        imp = dict(allow_small_or_imprecise_dtypes=True)
         g.iota(T.pi32[:, :], [[0, 1]], 0, 1).then_inc(S.gi, 1)
-        g.iota(T.dm[0:16, :], [[0, 8], [1, 16]], 0, -1, allow_small_or_imprecise_dtypes=True).then_inc(S.gi, 1)
-        g.iota(T.jb[:, :], [[16, 128]], 0, 0, allow_small_or_imprecise_dtypes=True).then_inc(S.gi, 1)
-        g.iota(T.vhi[:, :], [[64, 4], [0, 64]], 0, 16, allow_small_or_imprecise_dtypes=True).then_inc(S.gi, 1)
-        g.iota(T.vlo[:, :], [[0, 4], [1, 64]], 1, 0, allow_small_or_imprecise_dtypes=True).then_inc(S.gi, 1)
+        g.iota(T.dm[0:16, :], [[0, 8], [1, 16]], 0, -1, **imp).then_inc(S.gi, 1)
+        g.iota(T.vh4[:, :], [[64, 4]], 0, 16, **imp).then_inc(S.gi, 1)
+        g.iota(T.vlo[:, :], [[0, 4], [1, 64]], 1, 0, **imp).then_inc(S.gj, 1)
+        g.iota(T.jb[:, :], [[16, 128]], 0, 0, **imp).then_inc(S.gk, 1)
+        V.memset(T.dw[:, NT:NT + SLOTS], 0.0).then_inc(S.dz, 1)
+        V.memset(T.one16[:, :], 1.0).then_inc(S.o16, 1)
         vinc(V.memset(T.mone[0:16, :], sg))
         vinc(V.memset(T.c16[:, :], -16.0))
-        vinc(V.memset(T.win[:, 0:X0], 0.0))
-        vinc(V.memset(T.sel[:, :], 0.0))
-        vinc(V.memset(T.dw[:, NT:NT + SLOTS], 0.0))
-        V.wait_ge(S.gi, 5)
-        vwait()
+        V.wait_ge(S.gi, 3)
         vinc(V.tensor_scalar(T.pm32[:, :], T.pi32[:, :], 15, None, A.bitwise_and))
-        vinc(V.tensor_copy(T.offp[:, 0:1], T.pi32[:, :]))
         vinc(V.tensor_scalar(T.md[0:16, :], T.dm[0:16, :], 0.0, -sg, A.is_le, A.mult))
         vinc(V.tensor_scalar(T.mr[0:16, :], T.dm[0:16, :], 0.0, None, A.is_equal))
-        for q in range(8):
-            vinc(V.memset(T.sel[:, 16 * q:16 * q + 129 * 15 + 1:129], 1.0))
         vwait()
-        vinc(V.tensor_copy(T.pmf[:, :], T.pm32[:, :]))
-        vinc(V.tensor_scalar(T.initc[:, :], T.pm32[:, :], -1.0, float(cb + 16), A.mult, A.add))
         vinc(V.tensor_scalar(T.m0[:, :], T.pm32[:, :], 0.0, None, A.is_equal))
         vinc(V.tensor_scalar(T.m1[:, :], T.pm32[:, :], 1.0, None, A.is_equal))
-        V.wait_ge(S.kl, 16)
+        vinc(V.tensor_copy(T.pmf[:, :], T.pm32[:, :]))
+        vinc(V.tensor_scalar(T.initc[:, :], T.pm32[:, :], -1.0, float(cb + 16), A.mult, A.add))
         vwait()
+        V.wait_ge(S.kl, 16)
         vinc(V.tensor_copy(T.kb[0:16, :], T.ki[0:16, :]))
-        kb_at = vn[0]
-        PE.wait_ge(S.v, kb_at)
+        PE.wait_ge(S.v, vn[0])
         PE.matmul(T.ps5[:, 0:128], T.mone[0:16, :], T.kb[0:16, :], True, True).then_inc(S.p1, 1)
         PE.matmul(T.ps6[:, 0:128], T.md[0:16, :], T.kb[0:16, :], True, True).then_inc(S.p1, 1)
         PE.matmul(T.ps7[:, 0:128], T.mr[0:16, :], T.kb[0:16, :], True, True).then_inc(S.p1, 1)
         vwait()
-        V.wait_ge(S.p1, 3)
-        vinc(V.tensor_tensor_scan(T.sc[:, :], T.ps5[:, 0:128], T.c16[:, :], T.initc[:, 0:1], A.add, A.add))
+        V.wait_ge(S.gk, 1)
         vinc(V.tensor_scalar(T.jj[:, :], T.jb[:, :], T.pmf[:, 0:1], None, A.add))
+        vinc(V.tensor_scalar(T.vhm[:, :], T.vh4[:, :], T.m0[:, 0:1], None, A.mult))
+        vinc(V.tensor_copy(T.offp[:, 0:1], T.pi32[:, :]))
+        vinc(V.memset(T.win[:, 0:X0], 0.0))
+        vhm_at = vn[0]
+        vwait()
+        V.wait_ge(S.p1, 3)
+        V.wait_ge(S.dz, 1)
+        SC.wait_ge(S.dz, 1)
+        SC.activation(T.sel[:, :], T.dw[:, NT:NT + SLOTS], COPY).then_inc(S.selz, 1)
+        SC.wait_ge(S.selz, 1)
+        SC.wait_ge(S.o16, 1)
+        for q in range(8):
+            SC.activation(T.sel[:, 16 * q:16 * q + 129 * 15 + 1:129], T.one16[:, :], COPY).then_inc(S.selr, 1)
+        SC.wait_ge(S.gj, 1)
+        SC.wait_ge(S.v, vhm_at)
+        for u in range(4):
+            SC.activation(T.val[:, 64 * u:64 * u + 64], T.vlo[:, 64 * u:64 * u + 64], IDENT, bias=T.vhm[:, u:u + 1],
+                          scale=T.m1[:, 0:1]).then_inc(S.vab, 1)
+        vinc(V.tensor_tensor_scan(T.sc[:, :], T.ps5[:, 0:128], T.c16[:, :], T.initc[:, 0:1], A.add, A.add))
         vwait()
         vinc(V.tensor_tensor(T.t2[:, :], T.sc[:, :], T.ps6[:, 0:128], A.add))
-        vinc(V.tensor_scalar(T.va[:, :], T.vhi[:, :], T.m0[:, 0:1], None, A.mult))
-        vinc(V.tensor_scalar(T.vb[:, :], T.vlo[:, :], T.m1[:, 0:1], None, A.mult))
         vwait()
         vinc(V.tensor_tensor(T.t3[:, :], T.t2[:, :], T.ps7[:, 0:128], A.mult))
-        vinc(V.tensor_tensor(T.val[:, :], T.va[:, :], T.vb[:, :], A.add))
         vwait()
         vinc(V.tensor_tensor(T.pos[:, :], T.t3[:, :], T.jj[:, :], A.add))
         vwait()
         vinc(V.tensor_copy(T.o8[:, :], T.pos[:, :].indirect(T.offp[:, 0:1])))
         vwait()
+        V.wait_ge(S.selz, 1)
+        V.wait_ge(S.vab, 4)
         vinc(V.tensor_copy(T.dw[:, :].indirect(T.o8[:, :]), T.val[:, :]))
+        halves = (64, 0) if low else (0, 64)
+        PE.wait_ge(S.selr, 8)
         PE.wait_ge(S.v, vn[0])
-        for a in range(16):
-            mm = PE.matmul(T.ps4[:, 0:128], T.sel[:, 128 * a:128 * a + 128], T.dw[:, NT + a:NT + SLOTS:16], a == 0, a == 15)
-        mm.then_inc(S.p2, 1)
+        for ps, h0, sm in ((T.ps4, halves[0], S.p2a), (T.ps3, halves[1], S.p2b)):
+            for a in range(16):
+                s0 = NT + 16 * h0 + a
+                mm = PE.matmul(ps[:, 0:64], T.sel[:, 128 * a:128 * a + 128], T.dw[:, s0:s0 + 16 * 63 + 1:16], a == 0, a == 15)
+            mm.then_inc(sm, 1)
         vwait()
-        V.wait_ge(S.p2, 1)
-        vinc(V.tensor_copy(T.offs[:, :], T.ps4[:, 0:128]))
-        offs_at = vn[0]
-        vwait()
-        V.wait_ge(S.xl, 32)
-        g.scalar.wait_ge(S.v, offs_at)
-        g.scalar.wait_ge(S.xl, 32)
-        peer_half = SLOTS // 2 if low else 0
-        own_half = SLOTS // 2 - peer_half
         src = T.win[:, X0 - 1:X0 + NT]
-        for i, base in enumerate((peer_half, own_half)):
-            b, c = base, base + 512
-            V.tensor_copy(T.xc[:, b:b + 512], src.indirect(T.offs[:, b // 16:b // 16 + 32])).then_inc(S["gv%d" % i], 1)
-            g.scalar.activation(T.xc[:, c:c + 512], src.indirect(T.offs[:, c // 16:c // 16 + 32]),
-                                ActivationFunctionType.Copy).then_inc(S["gs%d" % i], 1)
-        snt_used = []
+        V.wait_ge(S.xl, 32)
+        SC.wait_ge(S.xl, 32)
+        for i, (ps, pe_sem, osem) in enumerate(((T.ps4, S.p2a, S.offa), (T.ps3, S.p2b, S.offb))):
+            h0 = halves[i]
+            V.wait_ge(pe_sem, 1)
+            V.tensor_copy(T.offs[:, h0:h0 + 64], ps[:, 0:64]).then_inc(osem, 1)
+            V.wait_ge(osem, 1)
+            SC.wait_ge(osem, 1)
+            b, c = 16 * h0, 16 * h0 + 512
+            V.tensor_copy(T.xc[:, b:b + 512], src.indirect(T.offs[:, h0:h0 + 32])).then_inc(S["gv%d" % i], 1)
+            SC.activation(T.xc[:, c:c + 512], src.indirect(T.offs[:, h0 + 32:h0 + 64]), COPY).then_inc(S["gs%d" % i], 1)
 
         def send(k):
             g.wait_ge(S["ld%d" % k], 32)
@@ -202,17 +220,23 @@ def rank_program(g, core, T, topo):
             g.remote_dma_fused(ts, local_sem=S.tsent)
             return len(ts)
 
-        send(0)
+        for k in range(PRE):
+            send(k)
         g.wait_ge(S.gv0, 1)
         g.wait_ge(S.gs0, 1)
         nt = tok(chip_of[peer], off)
         g.wait_ge(S.gv1, 1)
         g.wait_ge(S.gs1, 1)
         nt += tok(far + near, on_rest[0::2] + on_rest[1::2])
-        for k in range(1, CH // 2):
+        g.sem_inc(S.go, 1)
+        for k in range(PRE, CH // 2):
             send(k)
+        g.sync.wait_ge(S.go, 1)
+        gated = []
         for k in range(3, CH // 2):
-            g.sync.wait_ge(S["snt%d" % (k - 2)], 16)
+            if k - GATE >= PRE:
+                g.sync.wait_ge(S["snt%d" % (k - GATE)], 16)
+                gated.append(k - GATE)
             load(k, g.sync, g.sync)
         V.wait_ge(S.gv1, 1)
         V.wait_ge(S.gs1, 1)
@@ -238,8 +262,6 @@ def rank_program(g, core, T, topo):
         V.tensor_tensor(T.xs[:, :], T.xin[:, 0, :], T.xin[:, 1, :], A.add).then_inc(S.xsr, 1)
 
     PE.wait_ge(S.xsr, 1)
-    l1 = (S.l1a, S.l1b)
-    hs = (S.ha, S.hb)
 
     def layer1(c):
         if is_rank:
@@ -248,52 +270,70 @@ def rank_program(g, core, T, topo):
             PE.wait_ge(S["w%d" % c], len(on_a))
         ps = T["ps%d" % (c % 4)]
         PE.matmul(ps[:, 0:128], T.wbuf[:, c, 0:128], T.xs[:, :], True, True)
-        PE.matmul(ps[:, 128:256], T.wbuf[:, c, 128:256], T.xs[:, :], True, True).then_inc(l1[c % 2], 1)
-        V.wait_ge(l1[c % 2], c // 2 + 1)
-        V.tensor_scalar(T.hid[:, 256 * c:256 * c + 256], ps[:, 0:256], 0.0, None, A.max).then_inc(hs[c % 2], 1)
+        PE.matmul(ps[:, 128:256], T.wbuf[:, c, 128:256], T.xs[:, :], True, True).then_inc(S["l1_%d" % (c % 4)], 1)
+        V.wait_ge(S["l1_%d" % (c % 4)], c // 4 + 1)
+        V.tensor_scalar(T.hid[:, 256 * c:256 * c + 256], ps[:, 0:256], 0.0, None, A.max).then_inc(S["h_%d" % (c % 4)], 1)
+
+    acc = (T.ps4, T.ps5)
+
+    def layer2(c, hs):
+        PE.wait_ge(S["h_%d" % (c % 4)], c // 4 + 1)
+        for i in (0, 1):
+            for h in hs:
+                b = 256 * c + 128 * i + HP * h
+                mm = PE.matmul(acc[h][:, 0:HP], T.wbuf[:, c, 256 + 128 * i:384 + 128 * i], T.hid[:, b:b + HP],
+                               c == 0 and i == 0, c == CH - 1 and i == 1)
+        return mm
 
     layer1(0)
-    for c in range(CH):
-        if c + 1 < CH:
-            layer1(c + 1)
-        PE.wait_ge(hs[c % 2], c // 2 + 1)
-        for i in (0, 1):
-            mm = PE.matmul(T.ps4[:, 0:128], T.wbuf[:, c, 256 + 128 * i:384 + 128 * i],
-                           T.hid[:, 256 * c + 128 * i:256 * c + 128 * i + 128], c == 0 and i == 0, c == CH - 1 and i == 1)
-    mm.then_inc(S.acc, 1)
+    for c in range(CH - LATE):
+        layer1(c + 1)
+        layer2(c, (0, 1))
+    for c in range(CH - LATE + 1, CH):
+        layer1(c)
+    done = (S.acca, S.accb)
+    for h in (0, 1):
+        for c in range(CH - LATE, CH):
+            mm = layer2(c, (h,))
+        mm.then_inc(done[h], 1)
 
-    V.wait_ge(S.acc, 1)
-    out = res_slot(w) if is_rank else T.outr[:, :]
-    V.tensor_copy(out, T.ps4[:, 0:128]).then_inc(S.rdy, 1)
-    g.wait_ge(S.rdy, 1)
-    other = peer
+    ns = 0
+    for h in (0, 1):
+        rdy = (S.rdya, S.rdyb)[h]
+        there = T.win[:, R0 + w * PER + HP * h:R0 + w * PER + HP * h + HP]
+        out = there if is_rank else (T.out0, T.out1)[h][:, :]
+        V.wait_ge(done[h], 1)
+        V.tensor_copy(out, acc[h][:, 0:HP]).then_inc(rdy, 1)
+        g.wait_ge(rdy, 1)
+        ts = [tr(out, [(peer, there)], off, S.res)]
+        if not is_rank:
+            ts.append(tr(out, [(home, there)], on_rest, S.res))
+        g.remote_dma_fused(ts, local_sem=S.rsent)
+        ns += len(off) + (0 if is_rank else len(on_rest))
+    g.wait_ge(S.rsent, ns)
     if is_rank:
-        g.remote_dma_fused([tr(out, [(other, res_slot(w))], off, S.res)], local_sem=S.rsent)
-        g.wait_ge(S.rsent, len(off))
         g.wait_ge(S.tsent, nt)
-        for k in [0] + list(range(CH // 2 - 2, CH // 2)):
-            g.wait_ge(S["snt%d" % k], 16)
-        total = 7 * len(on_rest) + 8 * len(off)
+        for k in range(CH // 2):
+            if k not in gated:
+                g.wait_ge(S["snt%d" % k], 16)
+        total = 2 * (7 * len(on_rest) + 8 * len(off))
         yw = T.win[:, X0:X0 + NT + SLOTS]
-        V.wait_ge(S.res, total)
-        V.wait_ge(S.rdy, 1)
-        g.scalar.wait_ge(S.res, total)
-        g.scalar.wait_ge(S.rdy, 1)
-        g.scalar.wait_ge(S.v, vn[0])
-        for i in (0, 1):
-            b, c = 512 * i, 1024 + 512 * i
-            V.tensor_copy(T.ysb[:, b:b + 512], yw.indirect(T.posu[:, b // 16:b // 16 + 32])).then_inc(S["fv%d" % i], 1)
-            g.scalar.activation(T.ysb[:, c:c + 512], yw.indirect(T.posu[:, c // 16:c // 16 + 32]),
-                                ActivationFunctionType.Copy).then_inc(S["fs%d" % i], 1)
-        for i in (0, 1):
-            b, c = 512 * i, 1024 + 512 * i
+        for q in (V, SC):
+            q.wait_ge(S.res, total)
+            q.wait_ge(S.rdya, 1)
+            q.wait_ge(S.rdyb, 1)
+            q.wait_ge(S.v, vn[0])
+        np_ = NT // 2 // YP
+        for i in range(np_):
+            b, c = YP * i, NT // 2 + YP * i
+            V.tensor_copy(T.ysb[:, b:b + YP], yw.indirect(T.posu[:, b // 16:(b + YP) // 16])).then_inc(S["fv%d" % i], 1)
+            SC.activation(T.ysb[:, c:c + YP], yw.indirect(T.posu[:, c // 16:(c + YP) // 16]), COPY).then_inc(S["fs%d" % i], 1)
+        for i in range(np_):
+            b, c = YP * i, NT // 2 + YP * i
             g.sync.wait_ge(S["fv%d" % i], 1)
-            g.sync.dma_start(T.y[:, b:b + 512], T.ysb[:, b:b + 512]).then_inc(S.ys, 16)
+            g.sync.dma_start(T.y[:, b:b + YP], T.ysb[:, b:b + YP]).then_inc(S.ys, 16)
             g.sync.wait_ge(S["fs%d" % i], 1)
-            g.sync.dma_start(T.y[:, c:c + 512], T.ysb[:, c:c + 512]).then_inc(S.ys, 16)
-        g.sync.wait_ge(S.ys, 64)
-    else:
-        g.remote_dma_fused([tr(out, [(other, res_slot(w))], off, S.res),
-                            tr(out, [(home, res_slot(w))], on_rest, S.res)], local_sem=S.rsent)
-        g.wait_ge(S.rsent, len(off) + len(on_rest))
+            g.sync.dma_start(T.y[:, c:c + YP], T.ysb[:, c:c + YP]).then_inc(S.ys, 16)
+        g.sync.wait_ge(S.ys, 32 * np_)
+    elif n:
         g.wait_ge(S.fsent, n)

from concourse.bass import DstId, RemoteDMATransfer
from concourse.mybir import dt, AluOpType, ActivationFunctionType

NCORES = 256
SLOTS, PER, NT = 2048, 128, 2048
HP = PER // 2
CH = 16
PRE = 2
GATE = 2
LATE = 3
X0 = 4
YP = 512

SCRATCH = {
    "wbuf": ("sbuf", [128, CH, 512], "float32"),
    "win": ("sbuf", [128, X0 + NT + SLOTS], "float32"),
    "xc": ("sbuf", [128, SLOTS], "float32"),
    "ysb": ("sbuf", [128, NT], "float32"),
    "xin": ("sbuf", [128, 2, PER], "float32"),
    "xs": ("sbuf", [128, PER], "float32"),
    "hid": ("sbuf", [128, CH * 256], "float32"),
    "out0": ("sbuf", [128, HP], "float32"), "out1": ("sbuf", [128, HP], "float32"),
    "ki": ("sbuf", [128, 128], "int32"), "kb": ("sbuf", [128, 128], "bfloat16"),
    "pi32": ("sbuf", [128, 1], "int32"), "pm32": ("sbuf", [128, 1], "int32"),
    "pmf": ("sbuf", [128, 1], "float32"), "initc": ("sbuf", [128, 1], "float32"),
    "m0": ("sbuf", [128, 1], "float32"), "m1": ("sbuf", [128, 1], "float32"),
    "vh4": ("sbuf", [128, 4], "float32"), "vhm": ("sbuf", [128, 4], "float32"),
    "offp": ("sbuf", [128, 2], "uint16"), "o8": ("sbuf", [128, 16], "uint16"),
    "offs": ("sbuf", [128, 128], "uint16"), "posu": ("sbuf", [128, 128], "uint16"),
    "dm": ("sbuf", [128, 128], "float32"), "jb": ("sbuf", [128, 128], "float32"), "jj": ("sbuf", [128, 128], "float32"),
    "c16": ("sbuf", [128, 128], "float32"), "sc": ("sbuf", [128, 128], "float32"), "t2": ("sbuf", [128, 128], "float32"),
    "t3": ("sbuf", [128, 128], "float32"), "pos": ("sbuf", [128, 128], "float32"),
    "mone": ("sbuf", [128, 128], "bfloat16"), "md": ("sbuf", [128, 128], "bfloat16"), "mr": ("sbuf", [128, 128], "bfloat16"),
    "vlo": ("sbuf", [128, 256], "bfloat16"), "val": ("sbuf", [128, 256], "bfloat16"),
    "one16": ("sbuf", [128, 16], "bfloat16"),
    "sel": ("sbuf", [128, 16 * 128], "bfloat16"),
    "dw": ("sbuf", [128, NT + SLOTS], "bfloat16"),
}
for _k in range(8):
    SCRATCH["ps%d" % _k] = ("psum", [128, 512], "float32")

SEMAPHORES = (["go", "gi", "gj", "gk", "v", "p1", "p2a", "p2b", "kl", "xl", "dz", "o16", "vab", "selz", "selr", "offa",
               "offb", "tl", "th", "tsent", "gv0", "gv1", "gs0", "gs1", "xsr", "l1_0", "l1_1", "l1_2", "l1_3",
               "h_0", "h_1", "h_2", "h_3", "acca", "accb", "rdya", "rdyb", "rsent", "res", "ys", "fsent"]
              + ["fv%d" % k for k in range(4)] + ["fs%d" % k for k in range(4)]
              + ["ld%d" % k for k in range(CH // 2)] + ["snt%d" % k for k in range(CH // 2)]
              + ["w%d" % k for k in range(CH)])


def bits(mask):
    return [e for e in range(16) if (mask >> e) & 1]


def mask_of(engines):
    return sum(1 << e for e in engines)


def rank_program(g, core, T, topo):
    S = T.sem
    A = AluOpType
    COPY, IDENT = ActivationFunctionType.Copy, ActivationFunctionType.Identity

    def same_chip(a, b):
        return topo.host(a) == topo.host(b) and topo.chip(a) == topo.chip(b)

    home = [q for q in T.cores if same_chip(q, core)]
    if not home:
        return
    home = home[0]
    peer = [q for q in T.cores if topo.same_plane(home, q)][0]
    lo, hi = min(home, peer), max(home, peer)
    chip_of = {q: [c for c in range(NCORES) if same_chip(c, q)] for q in (lo, hi)}
    workers = chip_of[lo] + chip_of[hi]
    w = workers.index(core)
    mine = chip_of[home]
    near = [c for c in mine if c != home and topo.die(c) == topo.die(home)]
    far = [c for c in mine if topo.die(c) != topo.die(home)]
    is_rank = core == home
    carrier = [near[(c // 2) % len(near)] if c % 2 == 0 else far[(c // 2) % len(far)] for c in range(CH)]

    on = bits(topo.mask(core, [c for c in mine if c != core][0]))
    off = bits(topo.mask(core, peer))
    on_rest = [e for e in on if e not in off]
    on_a, on_b = on[0::2], on[1::2]

    def tr(src, dests, engines, sem):
        ids = []
        for d, _ in dests:
            rid, pid = topo.addr(d, core)
            ids.append(DstId(rid=rid, pnc=pid))
        return RemoteDMATransfer(dst_ids=ids, dma_engine_mask=mask_of(engines), remote_sem=sem,
                                 srcs=[src], dsts=[ap for _, ap in dests], alu_op=0)

    R0 = X0 + NT
    V = g.vector
    SC = g.scalar
    PE = g.tensor
    vn = [0]

    def vinc(call):
        call.then_inc(S.v, 1)
        vn[0] += 1

    def vwait():
        V.wait_ge(S.v, vn[0])

    if is_rank:
        low = core == lo
        sg = 1.0 if low else -1.0
        cb = SLOTS if low else 2 * SLOTS - 1
        g.sync.dma_start(T.ki[0:16, :], T.keep[:, :]).then_inc(S.kl, 16)

        def load(k, qa, qb):
            qa.dma_start(T.wbuf[:, 2 * k:2 * k + 2, 0:256], T.w1[:, 512 * k:512 * k + 512]).then_inc(S["ld%d" % k], 16)
            qb.dma_start(T.wbuf[:, 2 * k:2 * k + 2, 256:512], T.w2[:, 512 * k:512 * k + 512]).then_inc(S["ld%d" % k], 16)

        load(0, g.sync, SC)
        g.sync.dma_start(T.win[:, X0:X0 + NT // 2], T.x[:, 0:NT // 2]).then_inc(S.xl, 16)
        SC.dma_start(T.win[:, X0 + NT // 2:X0 + NT], T.x[:, NT // 2:NT]).then_inc(S.xl, 16)
        load(1, g.sync, g.sync)
        load(2, g.sync, g.sync)

        imp = dict(allow_small_or_imprecise_dtypes=True)
        g.iota(T.pi32[:, :], [[0, 1]], 0, 1).then_inc(S.gi, 1)
        g.iota(T.dm[0:16, :], [[0, 8], [1, 16]], 0, -1, **imp).then_inc(S.gi, 1)
        g.iota(T.vh4[:, :], [[64, 4]], 0, 16, **imp).then_inc(S.gi, 1)
        g.iota(T.vlo[:, :], [[0, 4], [1, 64]], 1, 0, **imp).then_inc(S.gj, 1)
        g.iota(T.jb[:, :], [[16, 128]], 0, 0, **imp).then_inc(S.gk, 1)
        V.memset(T.dw[:, NT:NT + SLOTS], 0.0).then_inc(S.dz, 1)
        V.memset(T.one16[:, :], 1.0).then_inc(S.o16, 1)
        vinc(V.memset(T.mone[0:16, :], sg))
        vinc(V.memset(T.c16[:, :], -16.0))
        V.wait_ge(S.gi, 3)
        vinc(V.tensor_scalar(T.pm32[:, :], T.pi32[:, :], 15, None, A.bitwise_and))
        vinc(V.tensor_scalar(T.md[0:16, :], T.dm[0:16, :], 0.0, -sg, A.is_le, A.mult))
        vinc(V.tensor_scalar(T.mr[0:16, :], T.dm[0:16, :], 0.0, None, A.is_equal))
        vwait()
        vinc(V.tensor_scalar(T.m0[:, :], T.pm32[:, :], 0.0, None, A.is_equal))
        vinc(V.tensor_scalar(T.m1[:, :], T.pm32[:, :], 1.0, None, A.is_equal))
        vinc(V.tensor_copy(T.pmf[:, :], T.pm32[:, :]))
        vinc(V.tensor_scalar(T.initc[:, :], T.pm32[:, :], -1.0, float(cb + 16), A.mult, A.add))
        vwait()
        V.wait_ge(S.kl, 16)
        vinc(V.tensor_copy(T.kb[0:16, :], T.ki[0:16, :]))
        PE.wait_ge(S.v, vn[0])
        PE.matmul(T.ps5[:, 0:128], T.mone[0:16, :], T.kb[0:16, :], True, True).then_inc(S.p1, 1)
        PE.matmul(T.ps6[:, 0:128], T.md[0:16, :], T.kb[0:16, :], True, True).then_inc(S.p1, 1)
        PE.matmul(T.ps7[:, 0:128], T.mr[0:16, :], T.kb[0:16, :], True, True).then_inc(S.p1, 1)
        vwait()
        V.wait_ge(S.gk, 1)
        vinc(V.tensor_scalar(T.jj[:, :], T.jb[:, :], T.pmf[:, 0:1], None, A.add))
        vinc(V.tensor_scalar(T.vhm[:, :], T.vh4[:, :], T.m0[:, 0:1], None, A.mult))
        vinc(V.tensor_copy(T.offp[:, 0:1], T.pi32[:, :]))
        vinc(V.memset(T.win[:, 0:X0], 0.0))
        vhm_at = vn[0]
        vwait()
        V.wait_ge(S.p1, 3)
        V.wait_ge(S.dz, 1)
        SC.wait_ge(S.dz, 1)
        SC.activation(T.sel[:, :], T.dw[:, NT:NT + SLOTS], COPY).then_inc(S.selz, 1)
        SC.wait_ge(S.selz, 1)
        SC.wait_ge(S.o16, 1)
        for q in range(8):
            SC.activation(T.sel[:, 16 * q:16 * q + 129 * 15 + 1:129], T.one16[:, :], COPY).then_inc(S.selr, 1)
        SC.wait_ge(S.gj, 1)
        SC.wait_ge(S.v, vhm_at)
        for u in range(4):
            SC.activation(T.val[:, 64 * u:64 * u + 64], T.vlo[:, 64 * u:64 * u + 64], IDENT, bias=T.vhm[:, u:u + 1],
                          scale=T.m1[:, 0:1]).then_inc(S.vab, 1)
        vinc(V.tensor_tensor_scan(T.sc[:, :], T.ps5[:, 0:128], T.c16[:, :], T.initc[:, 0:1], A.add, A.add))
        vwait()
        vinc(V.tensor_tensor(T.t2[:, :], T.sc[:, :], T.ps6[:, 0:128], A.add))
        vwait()
        vinc(V.tensor_tensor(T.t3[:, :], T.t2[:, :], T.ps7[:, 0:128], A.mult))
        vwait()
        vinc(V.tensor_tensor(T.pos[:, :], T.t3[:, :], T.jj[:, :], A.add))
        vwait()
        vinc(V.tensor_copy(T.o8[:, :], T.pos[:, :].indirect(T.offp[:, 0:1])))
        vwait()
        V.wait_ge(S.selz, 1)
        V.wait_ge(S.vab, 4)
        vinc(V.tensor_copy(T.dw[:, :].indirect(T.o8[:, :]), T.val[:, :]))
        halves = (64, 0) if low else (0, 64)
        PE.wait_ge(S.selr, 8)
        PE.wait_ge(S.v, vn[0])
        for ps, h0, sm in ((T.ps4, halves[0], S.p2a), (T.ps3, halves[1], S.p2b)):
            for a in range(16):
                s0 = NT + 16 * h0 + a
                mm = PE.matmul(ps[:, 0:64], T.sel[:, 128 * a:128 * a + 128], T.dw[:, s0:s0 + 16 * 63 + 1:16], a == 0, a == 15)
            mm.then_inc(sm, 1)
        vwait()
        src = T.win[:, X0 - 1:X0 + NT]
        V.wait_ge(S.xl, 32)
        SC.wait_ge(S.xl, 32)
        for i, (ps, pe_sem, osem) in enumerate(((T.ps4, S.p2a, S.offa), (T.ps3, S.p2b, S.offb))):
            h0 = halves[i]
            V.wait_ge(pe_sem, 1)
            V.tensor_copy(T.offs[:, h0:h0 + 64], ps[:, 0:64]).then_inc(osem, 1)
            V.wait_ge(osem, 1)
            SC.wait_ge(osem, 1)
            b, c = 16 * h0, 16 * h0 + 512
            V.tensor_copy(T.xc[:, b:b + 512], src.indirect(T.offs[:, h0:h0 + 32])).then_inc(S["gv%d" % i], 1)
            SC.activation(T.xc[:, c:c + 512], src.indirect(T.offs[:, h0 + 32:h0 + 64]), COPY).then_inc(S["gs%d" % i], 1)

        def send(k):
            g.wait_ge(S["ld%d" % k], 32)
            c0, c1 = 2 * k, 2 * k + 1
            g.remote_dma_fused([tr(T.wbuf[:, c0, :], [(carrier[c0], T.wbuf[:, c0, :])], on_b, S["w%d" % c0]),
                                tr(T.wbuf[:, c1, :], [(carrier[c1], T.wbuf[:, c1, :])], on_a, S["w%d" % c1])],
                               local_sem=S["snt%d" % k])

        half = 0 if low else 1
        tsem = S.tl if low else S.th

        def tok(dests, engines):
            ts = []
            for d, e in zip(dests, engines):
                i = workers.index(d)
                ts.append(tr(T.xc[:, i * PER:(i + 1) * PER], [(d, T.xin[:, half, :])], [e], tsem))
            g.remote_dma_fused(ts, local_sem=S.tsent)
            return len(ts)

        for k in range(PRE):
            send(k)
        g.wait_ge(S.gv0, 1)
        g.wait_ge(S.gs0, 1)
        nt = tok(chip_of[peer], off)
        g.wait_ge(S.gv1, 1)
        g.wait_ge(S.gs1, 1)
        nt += tok(far + near, on_rest[0::2] + on_rest[1::2])
        g.sem_inc(S.go, 1)
        for k in range(PRE, CH // 2):
            send(k)
        g.sync.wait_ge(S.go, 1)
        gated = []
        for k in range(3, CH // 2):
            if k - GATE >= PRE:
                g.sync.wait_ge(S["snt%d" % (k - GATE)], 16)
                gated.append(k - GATE)
            load(k, g.sync, g.sync)
        V.wait_ge(S.gv1, 1)
        V.wait_ge(S.gs1, 1)
        vinc(V.tensor_copy(T.posu[:, :], T.pos[:, :]))
        V.wait_ge(S.th if low else S.tl, 1)
        V.tensor_tensor(T.xs[:, :], T.xc[:, w * PER:(w + 1) * PER], T.xin[:, 1 - half, :], A.add).then_inc(S.xsr, 1)
        vwait()
    else:
        n = 0
        for c in range(CH):
            if carrier[c] != core:
                continue
            g.wait_ge(S["w%d" % c], len(on_a))
            rest = [d for d in mine if d not in (core, home)]
            a = [d for d in rest if topo.die(d) != topo.die(core)]
            b = [d for d in rest if topo.die(d) == topo.die(core)]
            ap = T.wbuf[:, c, :]
            g.remote_dma_fused([tr(ap, [(d, ap) for d in a], on_a, S["w%d" % c]),
                                tr(ap, [(d, ap) for d in b], on_b, S["w%d" % c])], local_sem=S.fsent)
            n += len(on_a) + len(on_b)
        V.wait_ge(S.tl, 1)
        V.wait_ge(S.th, 1)
        V.tensor_tensor(T.xs[:, :], T.xin[:, 0, :], T.xin[:, 1, :], A.add).then_inc(S.xsr, 1)

    PE.wait_ge(S.xsr, 1)

    def layer1(c):
        if is_rank:
            PE.wait_ge(S["ld%d" % (c // 2)], 32)
        else:
            PE.wait_ge(S["w%d" % c], len(on_a))
        ps = T["ps%d" % (c % 4)]
        PE.matmul(ps[:, 0:128], T.wbuf[:, c, 0:128], T.xs[:, :], True, True)
        PE.matmul(ps[:, 128:256], T.wbuf[:, c, 128:256], T.xs[:, :], True, True).then_inc(S["l1_%d" % (c % 4)], 1)
        V.wait_ge(S["l1_%d" % (c % 4)], c // 4 + 1)
        V.tensor_scalar(T.hid[:, 256 * c:256 * c + 256], ps[:, 0:256], 0.0, None, A.max).then_inc(S["h_%d" % (c % 4)], 1)

    acc = (T.ps4, T.ps5)

    def layer2(c, hs):
        PE.wait_ge(S["h_%d" % (c % 4)], c // 4 + 1)
        for i in (0, 1):
            for h in hs:
                b = 256 * c + 128 * i + HP * h
                mm = PE.matmul(acc[h][:, 0:HP], T.wbuf[:, c, 256 + 128 * i:384 + 128 * i], T.hid[:, b:b + HP],
                               c == 0 and i == 0, c == CH - 1 and i == 1)
        return mm

    layer1(0)
    for c in range(CH - LATE):
        layer1(c + 1)
        layer2(c, (0, 1))
    for c in range(CH - LATE + 1, CH):
        layer1(c)
    done = (S.acca, S.accb)
    for h in (0, 1):
        for c in range(CH - LATE, CH):
            mm = layer2(c, (h,))
        mm.then_inc(done[h], 1)

    ns = 0
    for h in (0, 1):
        rdy = (S.rdya, S.rdyb)[h]
        there = T.win[:, R0 + w * PER + HP * h:R0 + w * PER + HP * h + HP]
        out = there if is_rank else (T.out0, T.out1)[h][:, :]
        V.wait_ge(done[h], 1)
        V.tensor_copy(out, acc[h][:, 0:HP]).then_inc(rdy, 1)
        g.wait_ge(rdy, 1)
        ts = [tr(out, [(peer, there)], off, S.res)]
        if not is_rank:
            ts.append(tr(out, [(home, there)], on_rest, S.res))
        g.remote_dma_fused(ts, local_sem=S.rsent)
        ns += len(off) + (0 if is_rank else len(on_rest))
    g.wait_ge(S.rsent, ns)
    if is_rank:
        g.wait_ge(S.tsent, nt)
        for k in range(CH // 2):
            if k not in gated:
                g.wait_ge(S["snt%d" % k], 16)
        total = 2 * (7 * len(on_rest) + 8 * len(off))
        yw = T.win[:, X0:X0 + NT + SLOTS]
        for q in (V, SC):
            q.wait_ge(S.res, total)
            q.wait_ge(S.rdya, 1)
            q.wait_ge(S.rdyb, 1)
            q.wait_ge(S.v, vn[0])
        np_ = NT // 2 // YP
        for i in range(np_):
            b, c = YP * i, NT // 2 + YP * i
            V.tensor_copy(T.ysb[:, b:b + YP], yw.indirect(T.posu[:, b // 16:(b + YP) // 16])).then_inc(S["fv%d" % i], 1)
            SC.activation(T.ysb[:, c:c + YP], yw.indirect(T.posu[:, c // 16:(c + YP) // 16]), COPY).then_inc(S["fs%d" % i], 1)
        for i in range(np_):
            b, c = YP * i, NT // 2 + YP * i
            g.sync.wait_ge(S["fv%d" % i], 1)
            g.sync.dma_start(T.y[:, b:b + YP], T.ysb[:, b:b + YP]).then_inc(S.ys, 16)
            g.sync.wait_ge(S["fs%d" % i], 1)
            g.sync.dma_start(T.y[:, c:c + YP], T.ysb[:, c:c + YP]).then_inc(S.ys, 16)
        g.sync.wait_ge(S.ys, 32 * np_)
    elif n:
        g.wait_ge(S.fsent, n)
